import numpy as np
import ml_dtypes


def mxq(x, axis, fmt="e4m3"):
    dtype, down = {"e4m3": (ml_dtypes.float8_e4m3fn, 7), "e5m2": (ml_dtypes.float8_e5m2, 14)}[fmt]
    v = np.moveaxis(np.asarray(x, np.float32).astype(ml_dtypes.bfloat16).astype(np.float64), axis, -1)
    blocks = v.reshape(v.shape[:-1] + (-1, 32))
    amax = np.abs(blocks).max(-1, keepdims=True)
    byte = np.maximum(np.where(amax > 0, np.frexp(amax)[1] - 1 + 127, 0) - down, 1)
    scale = np.exp2(byte - 127.0)
    codes = (blocks / scale).astype(np.float32).astype(dtype).astype(np.float64)
    return np.moveaxis((codes * scale).reshape(v.shape), -1, axis)


WIDE = False


def mx_kscale(k):
    if not WIDE:
        return np.ones(k)
    levels = np.array([30, -30])
    if k % 512:
        return np.exp2(np.random.permutation(np.resize(levels, k // 32))).repeat(32)
    a = np.empty((k // 512, 16))
    for p in range(k // 512):
        a[p, :8] = np.random.permutation(np.resize(levels, 8))
        for g in range(8):
            far = levels[np.abs(levels - a[p, g]) >= 10]
            a[p, g + 8] = far[np.random.randint(len(far))]
    return np.exp2(a.ravel()).repeat(32)


def f64(x):
    return np.asarray(x).astype(np.float64)


def striped(idx):
    return np.tile(np.asarray(idx).reshape(-1, 16).T, (8, 1)).astype(np.uint16)


def unstriped(offs):
    return offs[:16].T.reshape(-1).astype(np.int64)


def striped8(idx):
    return np.asarray(idx).reshape(8, -1, 16).transpose(0, 2, 1).reshape(128, -1).astype(np.uint16)


def unstriped8(offs):
    return offs.reshape(8, 16, -1).transpose(0, 2, 1).reshape(8, -1).astype(np.int64)


def pick8(x, idx, run):
    r = np.arange(len(x))
    return x[r[:, None], idx[r % (8 * run) // run]]


E2M1 = np.array([0.0, 0.5, 1.0, 1.5, 2.0, 3.0, 4.0, 6.0, -0.0, -0.5, -1.0, -1.5, -2.0, -3.0, -4.0, -6.0])


def pack_weight(w, fmt):
    k, n = w.shape
    w = f64(np.asarray(w, np.float32).astype(ml_dtypes.bfloat16)).reshape(k // 32, 32, n)
    amax = np.abs(w).max(1)
    if fmt in ("e4m3", "e5m2"):
        byte = np.frexp(amax)[1] - 1 + 127 - (7 if fmt == "e4m3" else 14)
    else:
        mant, ex = np.frexp(amax / 6.0)
        byte = np.where(mant > 0.5, ex, ex - 1) + 127
    byte = np.clip(np.where(amax > 0, byte, 1), 1, 254)
    scaled = (w * np.exp2(127.0 - byte)[:, None, :]).reshape(k, n).astype(np.float32)
    by_word = np.ascontiguousarray(scaled.reshape(k // 512, 128, 4, n).transpose(0, 1, 3, 2))
    if fmt in ("e4m3", "e5m2"):
        words = by_word.astype(ml_dtypes.float8_e4m3fn if fmt == "e4m3" else ml_dtypes.float8_e5m2).view(np.uint8)
    else:
        c = by_word.astype(ml_dtypes.float4_e2m1fn).view(np.uint8) & 0xF
        words = (c[..., 0::2] | (c[..., 1::2] << 4)).reshape(k // 512, 128, 2 * n)
    return np.ascontiguousarray(words), np.ascontiguousarray(byte.astype(np.uint8).reshape(k // 512, 16, n))


def unpack_weight(words, scales, fmt):
    g, _, n = scales.shape
    words = np.ascontiguousarray(words).reshape(g, 128, n, -1)
    if fmt in ("e4m3", "e5m2"):
        vals = words.view(ml_dtypes.float8_e4m3fn if fmt == "e4m3" else ml_dtypes.float8_e5m2).astype(np.float64)
    else:
        nib = np.empty((g, 128, n, 4), np.uint8)
        nib[..., 0::2] = words & 0xF
        nib[..., 1::2] = words >> 4
        vals = E2M1[nib]
    vals = vals * np.repeat(np.exp2(scales.astype(np.float64) - 127.0), 8, axis=1)[..., None]
    return vals.transpose(0, 1, 3, 2).reshape(g * 512, n)


K, T, J, R, F, Z, C, D, O, N, S = 512, 1024, 256, 512, 512, 1024, 512, 512, 128, 256, 1024


def setup_inputs():
    n = np.random.standard_normal
    idx = np.random.permutation(T)[:J]
    idx2 = np.random.permutation(Z)[:J]
    idx3 = np.stack([np.random.permutation(C)[:J] for _ in range(8)])
    idx4 = np.random.permutation(D)[:J]
    idx5 = np.random.permutation(C)[:O]
    idx6 = np.stack([np.random.permutation(D)[:O] for _ in range(8)])
    idx7 = np.random.permutation(S)[:N]
    fk = mx_kscale(K)
    ff = mx_kscale(F)
    fr = mx_kscale(R)
    xtp = pack_weight(n((K, T)) / fk[:, None], "e4m3")
    xop = pack_weight(n((F, Z)) / ff[:, None], "e2m1")
    wp = pack_weight(n((K, R)) * 1 / np.sqrt(K) * fk[:, None] * fr, "e2m1")
    w2p = pack_weight(n((K, R)) * 1 / np.sqrt(K) * fk[:, None] * fr, "e5m2")
    w0p = pack_weight(n((F, R)) * 1 / np.sqrt(F) * ff[:, None] * fr, "e5m2")
    vsp = pack_weight(n((R, S)) * 1 / np.sqrt(R) / fr[:, None], "e5m2")
    return {
        "xt_words": xtp[0],
        "xt_scales": xtp[1],
        "xo_words": xop[0],
        "xo_scales": xop[1],
        "w_words": wp[0],
        "w_scales": wp[1],
        "w2_words": w2p[0],
        "w2_scales": w2p[1],
        "w0_words": w0p[0],
        "w0_scales": w0p[1],
        "sa": (np.random.uniform(0.5, 1.6, (R, 1))).astype(np.float32),
        "sb": (np.random.uniform(0.5, 1.6, (R, 1))).astype(np.float32),
        "vs_words": vsp[0],
        "vs_scales": vsp[1],
        "offs": striped(idx),
        "offs2": striped(idx2),
        "offs3": striped8(idx3),
        "offs4": striped(idx4),
        "offs5": striped(idx5),
        "offs6": striped8(idx6),
        "offs7": striped(idx7),
    }


def reference(xt_words, xt_scales, xo_words, xo_scales, w_words, w_scales, w2_words, w2_scales, w0_words, w0_scales, sa, sb, vs_words, vs_scales, offs, offs2, offs3, offs4, offs5, offs6, offs7):
    idx = unstriped(offs)
    idx2 = unstriped(offs2)
    idx3 = unstriped8(offs3)
    idx4 = unstriped(offs4)
    idx5 = unstriped(offs5)
    idx6 = unstriped8(offs6)
    idx7 = unstriped(offs7)
    xtu = unpack_weight(xt_words, xt_scales, "e4m3")
    xou = unpack_weight(xo_words, xo_scales, "e2m1")
    wu = unpack_weight(w_words, w_scales, "e2m1")
    w2u = unpack_weight(w2_words, w2_scales, "e5m2")
    w0u = unpack_weight(w0_words, w0_scales, "e5m2")
    vsu = unpack_weight(vs_words, vs_scales, "e5m2")
    xtidxg = xtu[:, idx]
    a = wu.T @ xtidxg
    xoidx2g = xou[:, idx2]
    b = w2u.T @ xtidxg + w0u.T @ xoidx2g
    pw = np.zeros((R, C))
    pw[np.arange(R)[:, None], idx3[np.arange(R) % 512 // 64]] = a
    pv = np.zeros((R, D))
    pv[:, idx4] = b
    hid = np.maximum(pw[:, idx5] * f64(sa), pick8(pv, idx6, 64) * f64(sb))
    vsidx7g = vsu[:, idx7]
    hidq = mxq(hid, 0, "e4m3")
    y = vsidx7g.T @ hidq
    return y

@@ -1,0 +1,181 @@
+from contextlib import ExitStack
+
+import concourse.mybir as mybir
+
+F32 = mybir.dt.float32
+BF16 = mybir.dt.bfloat16
+I32 = mybir.dt.int32
+U32 = mybir.dt.uint32
+U16 = mybir.dt.uint16
+U8 = mybir.dt.uint8
+E4M3 = mybir.dt.float8_e4m3fn_x4
+E5M2 = mybir.dt.float8_e5m2_x4
+E2M1 = mybir.dt.float4_e2m1fn_x4
+COPY = mybir.ActivationFunctionType.Copy
+MAX = mybir.AluOpType.max
+
+P = 128
+PACK = 4
+T, J, R, Z, C, D, O, N, S = 1024, 256, 512, 1024, 512, 512, 128, 256, 1024
+FLOPS = 436207616
+
+
+def tile_list_owncommon_leaned_store_plain_kernel(
+    tc, xt_words, xt_scales, xo_words, xo_scales, w_words, w_scales, w2_words, w2_scales, w0_words, w0_scales,
+    sa, sb, vs_words, vs_scales, offs, offs2, offs3, offs4, offs5, offs6, offs7, out,
+):
+    nc = tc.nc
+    with ExitStack() as ctx:
+        keep = ctx.enter_context(tc.tile_pool(name="keep", bufs=1))
+        psum = ctx.enter_context(tc.psum_pool(name="psum", bufs=1))
+
+        def tile(name, width, dtype):
+            return keep.tile([P, width], dtype, name=name, align_bytes=64)
+
+        def load_list(name, src):
+            t = keep.tile([P, src.shape[1]], U16, name=name)
+            nc.sync.dma_start(t[:], src)
+            return t
+
+        def load_words8(name, src, width):
+            t = tile(name, width, U32)
+            nc.sync.dma_start(t[:].bitcast(I32), src[0].rearrange("p n t -> p (n t)").bitcast(I32))
+            return t
+
+        def load_words4(name, src, width):
+            t = tile(name, width, U16)
+            nc.sync.dma_start(t[:].bitcast(I32), src[0].bitcast(I32))
+            return t
+
+        def zeroed_plane(name, width, eng=nc.vector):
+            t = tile(name, width, U8)
+            eng.memset(t[:].bitcast(I32), 0)
+            return t
+
+        def load_plane(t, src, queue):
+            for q in range(4):
+                queue.dma_start(t[32 * q : 32 * q + 4, :].bitcast(I32), src[0, 4 * q : 4 * q + 4, :].bitcast(I32))
+
+        def gather(name, window, offsets, dtype):
+            t = tile(name, J, dtype)
+            nc.vector.tensor_copy(t[:], window[:].indirect(offsets[:]))
+            return t
+
+        def deal_words(name, src, dtype):
+            t = tile(name, R, dtype)
+            nc.scalar.copy(t[:].rearrange("p (t m) -> p m t", t=PACK), src[:].rearrange("p (m t) -> p m t", t=PACK))
+            return t
+
+        def deal_plane(name, src):
+            t = tile(name, R, U8)
+            nc.vector.tensor_copy(t[:].rearrange("p (t m) -> p t m", t=PACK), src[:].rearrange("p (m t) -> p t m", t=PACK))
+            return t
+
+        xt_s = zeroed_plane("xt_s", T)
+        w_s = zeroed_plane("w_s", R)
+        xo_s = zeroed_plane("xo_s", Z)
+        w2_s = zeroed_plane("w2_s", R)
+        w0_s = zeroed_plane("w0_s", R, nc.gpsimd)
+        vs_s = zeroed_plane("vs_s", S, nc.gpsimd)
+        pw = [tile("pw%d" % i, C, F32) for i in range(2)]
+        pv = [tile("pv%d" % i, D, F32) for i in range(4)]
+        for b in pw + pv:
+            nc.vector.memset(b[:], 0.0)
+
+        xt_w = load_words8("xt_w", xt_words, T)
+        load_plane(xt_s, xt_scales, nc.sync)
+        l1 = load_list("l1", offs)
+        w_w = load_words4("w_w", w_words, R)
+        load_plane(w_s, w_scales, nc.sync)
+        load_plane(w0_s, w0_scales, nc.gpsimd)
+        w2_w = load_words8("w2_w", w2_words, R)
+        w0_w = load_words8("w0_w", w0_words, R)
+        l3 = load_list("l3", offs3)
+        l2 = load_list("l2", offs2)
+        xo_w = load_words4("xo_w", xo_words, Z)
+        load_plane(xo_s, xo_scales, nc.sync)
+        load_plane(w2_s, w2_scales, nc.sync)
+        l4 = load_list("l4", offs4)
+        l5 = load_list("l5", offs5)
+        sa_t = keep.tile([P, PACK], F32, name="sa_t")
+        sb_t = keep.tile([P, PACK], F32, name="sb_t")
+        nc.sync.dma_start(sa_t[:], sa.rearrange("(p t) o -> p (t o)", t=PACK))
+        l6 = load_list("l6", offs6)
+        nc.sync.dma_start(sb_t[:], sb.rearrange("(p t) o -> p (t o)", t=PACK))
+        load_plane(vs_s, vs_scales, nc.gpsimd)
+        l7 = load_list("l7", offs7)
+        vs_w = load_words8("vs_w", vs_words, S)
+
+        w_wd = deal_words("w_wd", w_w, U16)
+        xt_sg = gather("xt_sg", xt_s, l1, U8)
+        xt_wg = gather("xt_wg", xt_w, l1, U32)
+        w_sd = deal_plane("w_sd", w_s)
+        w2_wd = deal_words("w2_wd", w2_w, U32)
+        w0_wd = deal_words("w0_wd", w0_w, U32)
+
+        a_ps = [psum.tile([P, J], F32, name="a_ps%d" % t, tag="bank%d" % t) for t in range(PACK)]
+        b_ps = [psum.tile([P, J], F32, name="b_ps%d" % t, tag="bank%d" % (PACK + t)) for t in range(PACK)]
+        for t in range(PACK):
+            cols = slice(P * t, P * (t + 1))
+            nc.tensor.matmul_mx(
+                out=a_ps[t][:], lhsT=w_wd[:, cols].bitcast(E2M1), lhsT_scale=w_sd[:, cols],
+                rhs=xt_wg[:].bitcast(E4M3), rhs_scale=xt_sg[:], start=True, stop=True,
+            )
+
+        xo_wg = gather("xo_wg", xo_w, l2, U16)
+        xo_sg = gather("xo_sg", xo_s, l2, U8)
+        w2_sd = deal_plane("w2_sd", w2_s)
+        w0_sd = deal_plane("w0_sd", w0_s)
+        for t in range(PACK):
+            cols = slice(P * t, P * (t + 1))
+            nc.tensor.matmul_mx(
+                out=b_ps[t][:], lhsT=w2_wd[:, cols].bitcast(E5M2), lhsT_scale=w2_sd[:, cols],
+                rhs=xt_wg[:].bitcast(E4M3), rhs_scale=xt_sg[:], start=True, stop=False,
+            )
+            nc.tensor.matmul_mx(
+                out=b_ps[t][:], lhsT=w0_wd[:, cols].bitcast(E5M2), lhsT_scale=w0_sd[:, cols],
+                rhs=xo_wg[:].bitcast(E2M1), rhs_scale=xo_sg[:], start=False, stop=True,
+            )
+
+        gw = [keep.tile([P, 2, O], F32, name="gw%d" % h) for h in range(2)]
+        gv = [keep.tile([P, 2, O], F32, name="gv%d" % h) for h in range(2)]
+        hid = keep.tile([P, O, PACK], BF16, name="hid", align_bytes=64)
+
+        for t in range(PACK):
+            a_sb = tile("a_sb%d" % t, J, F32)
+            nc.scalar.activation(a_sb[:], a_ps[t][:], COPY)
+            nc.scalar.activation(pw[t % 2][:].indirect(l3[:]), a_sb[:], COPY)
+            nc.scalar.activation(gw[t // 2][:, t % 2, :], pw[t % 2][:].indirect(l5[:]), COPY, scale=sa_t[:, t : t + 1])
+
+        for t in range(PACK):
+            b_sb = tile("b_sb%d" % t, J, F32)
+            nc.vector.tensor_copy(b_sb[:], b_ps[t][:])
+            nc.vector.tensor_copy(pv[t][:].indirect(l4[:]), b_sb[:])
+            nc.scalar.activation(gv[t // 2][:, t % 2, :], pv[t][:].indirect(l6[:]), COPY, scale=sb_t[:, t : t + 1])
+            if t == 1:
+                vs_wg = gather("vs_wg", vs_w, l7, U32)
+                vs_sg = gather("vs_sg", vs_s, l7, U8)
+            if t % 2 == 1:
+                h = t // 2
+                nc.vector.tensor_tensor(
+                    hid[:, :, 2 * h : 2 * h + 2], gw[h][:].rearrange("p t o -> p o t"), gv[h][:].rearrange("p t o -> p o t"), MAX
+                )
+
+        hid_w = tile("hid_w", O, U32)
+        hid_s = tile("hid_s", O, U8)
+        nc.vector.quantize_mx(out=hid_w[:].bitcast(E4M3), scales=hid_s[:], in_=hid[:].rearrange("p o t -> p (o t)"))
+
+        for h in range(2):
+            cols = slice(P * h, P * (h + 1))
+            y_ps = psum.tile([P, O], F32, name="y_ps%d" % h, tag="bank%d" % h)
+            nc.tensor.matmul_mx(
+                out=y_ps[:], lhsT=vs_wg[:, cols].bitcast(E5M2), lhsT_scale=vs_sg[:, cols],
+                rhs=hid_w[:].bitcast(E4M3), rhs_scale=hid_s[:], start=True, stop=True,
+            )
+            y_sb = tile("y_sb%d" % h, O, F32)
+            if h == 0:
+                nc.scalar.activation(y_sb[:], y_ps[:], COPY)
+                nc.scalar.dma_start(out[cols, :], y_sb[:])
+            else:
+                nc.vector.tensor_copy(y_sb[:], y_ps[:])
+                nc.sync.dma_start(out[cols, :], y_sb[:])

@@ -37,14 +37,14 @@ def tile_list_owncommon_leaned_store_plain_kernel(
             nc.sync.dma_start(t[:], src)
             return t
 
-        def load_words8(name, src, width):
-            t = tile(name, width, U32)
-            nc.sync.dma_start(t[:].bitcast(I32), src[0].rearrange("p n t -> p (n t)").bitcast(I32))
+        def load_words8(name, src, width, tag=None, queue=nc.sync):
+            t = keep.tile([P, width], U32, name=name, tag=tag or name, align_bytes=64)
+            queue.dma_start(t[:].bitcast(I32), src[0].rearrange("p n t -> p (n t)").bitcast(I32))
             return t
 
-        def load_words4(name, src, width):
+        def load_words4(name, src, width, queue=nc.sync):
             t = tile(name, width, U16)
-            nc.sync.dma_start(t[:].bitcast(I32), src[0].bitcast(I32))
+            queue.dma_start(t[:].bitcast(I32), src[0].bitcast(I32))
             return t
 
         def zeroed_plane(name, width, eng=nc.vector):
@@ -55,6 +55,16 @@ def tile_list_owncommon_leaned_store_plain_kernel(
         def load_plane(t, src, queue):
             for q in range(4):
                 queue.dma_start(t[32 * q : 32 * q + 4, :].bitcast(I32), src[0, 4 * q : 4 * q + 4, :].bitcast(I32))
+
+        def zeroed_halves(name):
+            t = tile(name, 2 * R, U8)
+            nc.vector.memset(t[0:64, :].bitcast(I32), 0)
+            return t
+
+        def load_halves(t, src):
+            rows = src[0].bitcast(I32).rearrange("(h q r) c -> q r h c", h=2, q=2)
+            for q in range(2):
+                nc.sync.dma_start(t[32 * q : 32 * q + 4, :].bitcast(I32).rearrange("p (h c) -> p h c", h=2), rows[q])
 
         def gather(name, window, offsets, dtype):
             t = tile(name, J, dtype)
@@ -68,43 +78,44 @@ def tile_list_owncommon_leaned_store_plain_kernel(
 
         def deal_plane(name, src):
             t = tile(name, R, U8)
-            nc.vector.tensor_copy(t[:].rearrange("p (t m) -> p t m", t=PACK), src[:].rearrange("p (m t) -> p t m", t=PACK))
+            nc.vector.tensor_copy(src[64:128, 0:R].bitcast(I32), src[0:64, R : 2 * R].bitcast(I32))
+            nc.vector.tensor_copy(t[:].rearrange("p (t m) -> p t m", t=PACK), src[:, 0:R].rearrange("p (m t) -> p t m", t=PACK))
             return t
 
         xt_s = zeroed_plane("xt_s", T)
-        w_s = zeroed_plane("w_s", R)
+        w_s = zeroed_halves("w_s")
+        w2_s = zeroed_halves("w2_s")
+        w0_s = zeroed_halves("w0_s")
         xo_s = zeroed_plane("xo_s", Z)
-        w2_s = zeroed_plane("w2_s", R)
-        w0_s = zeroed_plane("w0_s", R, nc.gpsimd)
-        vs_s = zeroed_plane("vs_s", S, nc.gpsimd)
+        vs_s = zeroed_plane("vs_s", S)
         pw = [tile("pw%d" % i, C, F32) for i in range(2)]
         pv = [tile("pv%d" % i, D, F32) for i in range(4)]
         for b in pw + pv:
             nc.vector.memset(b[:], 0.0)
 
-        xt_w = load_words8("xt_w", xt_words, T)
-        load_plane(xt_s, xt_scales, nc.sync)
-        l1 = load_list("l1", offs)
-        w_w = load_words4("w_w", w_words, R)
-        load_plane(w_s, w_scales, nc.sync)
-        load_plane(w0_s, w0_scales, nc.gpsimd)
-        w2_w = load_words8("w2_w", w2_words, R)
-        w0_w = load_words8("w0_w", w0_words, R)
-        l3 = load_list("l3", offs3)
-        l2 = load_list("l2", offs2)
-        xo_w = load_words4("xo_w", xo_words, Z)
-        load_plane(xo_s, xo_scales, nc.sync)
-        load_plane(w2_s, w2_scales, nc.sync)
-        l4 = load_list("l4", offs4)
-        l5 = load_list("l5", offs5)
         sa_t = keep.tile([P, PACK], F32, name="sa_t")
         sb_t = keep.tile([P, PACK], F32, name="sb_t")
-        nc.sync.dma_start(sa_t[:], sa.rearrange("(p t) o -> p (t o)", t=PACK))
-        l6 = load_list("l6", offs6)
-        nc.sync.dma_start(sb_t[:], sb.rearrange("(p t) o -> p (t o)", t=PACK))
-        load_plane(vs_s, vs_scales, nc.gpsimd)
-        l7 = load_list("l7", offs7)
+        nc.gpsimd.dma_start(sa_t[:], sa.rearrange("(p t) o -> p (t o)", t=PACK))
+        nc.gpsimd.dma_start(sb_t[:], sb.rearrange("(p t) o -> p (t o)", t=PACK))
+        l1 = load_list("l1", offs)
+        xt_w = load_words8("xt_w", xt_words, T)
+        load_plane(xt_s, xt_scales, nc.scalar)
+        load_halves(w_s, w_scales)
+        w_w = load_words4("w_w", w_words, R)
+        w2_w = load_words8("w2_w", w2_words, R)
+        l3 = load_list("l3", offs3)
+        w0_w = load_words8("w0_w", w0_words, R, "w0_w")
+        load_halves(w2_s, w2_scales)
+        load_halves(w0_s, w0_scales)
+        xo_w = load_words4("xo_w", xo_words, Z)
+        l2 = load_list("l2", offs2)
+        load_plane(xo_s, xo_scales, nc.sync)
         vs_w = load_words8("vs_w", vs_words, S)
+        load_plane(vs_s, vs_scales, nc.sync)
+        l7 = load_list("l7", offs7)
+        l4 = load_list("l4", offs4)
+        l5 = load_list("l5", offs5)
+        l6 = load_list("l6", offs6)
 
         w_wd = deal_words("w_wd", w_w, U16)
         xt_sg = gather("xt_sg", xt_s, l1, U8)
@@ -122,10 +133,12 @@ def tile_list_owncommon_leaned_store_plain_kernel(
                 rhs=xt_wg[:].bitcast(E4M3), rhs_scale=xt_sg[:], start=True, stop=True,
             )
 
-        xo_wg = gather("xo_wg", xo_w, l2, U16)
-        xo_sg = gather("xo_sg", xo_s, l2, U8)
         w2_sd = deal_plane("w2_sd", w2_s)
         w0_sd = deal_plane("w0_sd", w0_s)
+        xo_wg = gather("xo_wg", xo_w, l2, U16)
+        xo_sg = gather("xo_sg", xo_s, l2, U8)
+        vs_wg = gather("vs_wg", vs_w, l7, U32)
+        vs_sg = gather("vs_sg", vs_s, l7, U8)
         for t in range(PACK):
             cols = slice(P * t, P * (t + 1))
             nc.tensor.matmul_mx(
@@ -142,7 +155,7 @@ def tile_list_owncommon_leaned_store_plain_kernel(
         hid = keep.tile([P, O, PACK], BF16, name="hid", align_bytes=64)
 
         for t in range(PACK):
-            a_sb = tile("a_sb%d" % t, J, F32)
+            a_sb = keep.tile([P, J], F32, name="a_sb%d" % t, tag="w0_w" if t == 0 else "a_sb%d" % t, align_bytes=64)
             nc.scalar.activation(a_sb[:], a_ps[t][:], COPY)
             nc.scalar.activation(pw[t % 2][:].indirect(l3[:]), a_sb[:], COPY)
             nc.scalar.activation(gw[t // 2][:, t % 2, :], pw[t % 2][:].indirect(l5[:]), COPY, scale=sa_t[:, t : t + 1])
@@ -152,9 +165,6 @@ def tile_list_owncommon_leaned_store_plain_kernel(
             nc.vector.tensor_copy(b_sb[:], b_ps[t][:])
             nc.vector.tensor_copy(pv[t][:].indirect(l4[:]), b_sb[:])
             nc.scalar.activation(gv[t // 2][:, t % 2, :], pv[t][:].indirect(l6[:]), COPY, scale=sb_t[:, t : t + 1])
-            if t == 1:
-                vs_wg = gather("vs_wg", vs_w, l7, U32)
-                vs_sg = gather("vs_sg", vs_s, l7, U8)
             if t % 2 == 1:
                 h = t // 2
                 nc.vector.tensor_tensor(

@@ -73,7 +73,8 @@ def tile_list_owncommon_leaned_store_plain_kernel(
 
         def deal_words(name, src, dtype):
             t = tile(name, R, dtype)
-            nc.scalar.copy(t[:].rearrange("p (t m) -> p m t", t=PACK), src[:].rearrange("p (m t) -> p m t", t=PACK))
+            i = 4 if dtype == U32 else 8
+            nc.scalar.copy(t[:].rearrange("p (t m i) -> p m t i", t=PACK, i=i), src[:].rearrange("p (m i t) -> p m t i", t=PACK, i=i))
             return t
 
         def deal_plane(name, src):
@@ -82,8 +83,8 @@ def tile_list_owncommon_leaned_store_plain_kernel(
             nc.vector.tensor_copy(t[:].rearrange("p (t m) -> p t m", t=PACK), src[:, 0:R].rearrange("p (m t) -> p t m", t=PACK))
             return t
 
-        xt_s = zeroed_plane("xt_s", T)
         w_s = zeroed_halves("w_s")
+        xt_s = zeroed_plane("xt_s", T)
         w2_s = zeroed_halves("w2_s")
         w0_s = zeroed_halves("w0_s")
         xo_s = zeroed_plane("xo_s", Z)
@@ -91,36 +92,36 @@ def tile_list_owncommon_leaned_store_plain_kernel(
         pw = [tile("pw%d" % i, C, F32) for i in range(2)]
         pv = [tile("pv%d" % i, D, F32) for i in range(4)]
         for b in pw + pv:
-            nc.vector.memset(b[:], 0.0)
+            nc.vector.memset(b[:].bitcast(I32), 0)
 
         sa_t = keep.tile([P, PACK], F32, name="sa_t")
         sb_t = keep.tile([P, PACK], F32, name="sb_t")
-        nc.gpsimd.dma_start(sa_t[:], sa.rearrange("(p t) o -> p (t o)", t=PACK))
-        nc.gpsimd.dma_start(sb_t[:], sb.rearrange("(p t) o -> p (t o)", t=PACK))
         l1 = load_list("l1", offs)
-        xt_w = load_words8("xt_w", xt_words, T)
-        load_plane(xt_s, xt_scales, nc.scalar)
         load_halves(w_s, w_scales)
+        load_plane(xt_s, xt_scales, nc.scalar)
+        xt_w = load_words8("xt_w", xt_words, T)
         w_w = load_words4("w_w", w_words, R)
-        w2_w = load_words8("w2_w", w2_words, R)
-        l3 = load_list("l3", offs3)
-        w0_w = load_words8("w0_w", w0_words, R, "w0_w")
         load_halves(w2_s, w2_scales)
         load_halves(w0_s, w0_scales)
+        w2_w = load_words8("w2_w", w2_words, R)
+        w0_w = load_words8("w0_w", w0_words, R, "w0_w")
         xo_w = load_words4("xo_w", xo_words, Z)
+        l3 = load_list("l3", offs3)
         l2 = load_list("l2", offs2)
         load_plane(xo_s, xo_scales, nc.sync)
-        vs_w = load_words8("vs_w", vs_words, S)
-        load_plane(vs_s, vs_scales, nc.sync)
-        l7 = load_list("l7", offs7)
+        load_plane(vs_s, vs_scales, nc.gpsimd)
         l4 = load_list("l4", offs4)
+        vs_w = load_words8("vs_w", vs_words, S)
+        l7 = load_list("l7", offs7)
         l5 = load_list("l5", offs5)
+        nc.sync.dma_start(sa_t[:], sa.rearrange("(p t) o -> p (t o)", t=PACK))
         l6 = load_list("l6", offs6)
+        nc.sync.dma_start(sb_t[:], sb.rearrange("(p t) o -> p (t o)", t=PACK))
 
         w_wd = deal_words("w_wd", w_w, U16)
         xt_sg = gather("xt_sg", xt_s, l1, U8)
-        xt_wg = gather("xt_wg", xt_w, l1, U32)
         w_sd = deal_plane("w_sd", w_s)
+        xt_wg = gather("xt_wg", xt_w, l1, U32)
         w2_wd = deal_words("w2_wd", w2_w, U32)
         w0_wd = deal_words("w0_wd", w0_w, U32)
 
@@ -150,27 +151,29 @@ def tile_list_owncommon_leaned_store_plain_kernel(
                 rhs=xo_wg[:].bitcast(E2M1), rhs_scale=xo_sg[:], start=False, stop=True,
             )
 
-        gw = [keep.tile([P, 2, O], F32, name="gw%d" % h) for h in range(2)]
-        gv = [keep.tile([P, 2, O], F32, name="gv%d" % h) for h in range(2)]
+        gw = [tile("gw%d" % t, O, F32) for t in range(PACK)]
+        gv = [tile("gv%d" % t, O, F32) for t in range(PACK)]
+        hid_t = keep.tile([P, PACK, O], BF16, name="hid_t", align_bytes=64)
         hid = keep.tile([P, O, PACK], BF16, name="hid", align_bytes=64)
 
+        a_sb = keep.tile([P, 2 * J], F32, name="a_sb", tag="w0_w", align_bytes=64)
         for t in range(PACK):
-            a_sb = keep.tile([P, J], F32, name="a_sb%d" % t, tag="w0_w" if t == 0 else "a_sb%d" % t, align_bytes=64)
-            nc.scalar.activation(a_sb[:], a_ps[t][:], COPY)
-            nc.scalar.activation(pw[t % 2][:].indirect(l3[:]), a_sb[:], COPY)
-            nc.scalar.activation(gw[t // 2][:, t % 2, :], pw[t % 2][:].indirect(l5[:]), COPY, scale=sa_t[:, t : t + 1])
+            a_t = a_sb[:, (t % 2) * J : (t % 2 + 1) * J]
+            nc.scalar.activation(a_t, a_ps[t][:], COPY)
+            nc.scalar.activation(pw[t % 2][:].indirect(l3[:]), a_t, COPY)
+            nc.scalar.activation(gw[t][:], pw[t % 2][:].indirect(l5[:]), COPY, scale=sa_t[:, t : t + 1])
 
         for t in range(PACK):
             b_sb = tile("b_sb%d" % t, J, F32)
-            nc.vector.tensor_copy(b_sb[:], b_ps[t][:])
+            if t == PACK - 1:
+                nc.scalar.activation(b_sb[:], b_ps[t][:], COPY)
+            else:
+                nc.vector.tensor_copy(b_sb[:], b_ps[t][:])
             nc.vector.tensor_copy(pv[t][:].indirect(l4[:]), b_sb[:])
-            nc.scalar.activation(gv[t // 2][:, t % 2, :], pv[t][:].indirect(l6[:]), COPY, scale=sb_t[:, t : t + 1])
-            if t % 2 == 1:
-                h = t // 2
-                nc.vector.tensor_tensor(
-                    hid[:, :, 2 * h : 2 * h + 2], gw[h][:].rearrange("p t o -> p o t"), gv[h][:].rearrange("p t o -> p o t"), MAX
-                )
+            nc.scalar.activation(gv[t][:], pv[t][:].indirect(l6[:]), COPY, scale=sb_t[:, t : t + 1])
+            nc.vector.tensor_tensor(hid_t[:, t, :], gw[t][:], gv[t][:], MAX)
 
+        nc.vector.tensor_copy(hid[:], hid_t[:].rearrange("p t o -> p o t"))
         hid_w = tile("hid_w", O, U32)
         hid_s = tile("hid_s", O, U8)
         nc.vector.quantize_mx(out=hid_w[:].bitcast(E4M3), scales=hid_s[:], in_=hid[:].rearrange("p o t -> p (o t)"))

@@ -29,8 +29,8 @@ def tile_list_owncommon_leaned_store_plain_kernel(
         keep = ctx.enter_context(tc.tile_pool(name="keep", bufs=1))
         psum = ctx.enter_context(tc.psum_pool(name="psum", bufs=1))
 
-        def tile(name, width, dtype):
-            return keep.tile([P, width], dtype, name=name, align_bytes=64)
+        def tile(name, width, dtype, tag=None):
+            return keep.tile([P, width], dtype, name=name, tag=tag or name, align_bytes=64)
 
         def load_list(name, src):
             t = keep.tile([P, src.shape[1]], U16, name=name)
@@ -48,26 +48,29 @@ def tile_list_owncommon_leaned_store_plain_kernel(
             return t
 
         def zeroed_plane(name, width, eng=nc.vector):
-            t = tile(name, width, U8)
+            t = tile(name, width + 4, U8)
             eng.memset(t[:].bitcast(I32), 0)
             return t
 
-        def load_plane(t, src, queue):
-            for q in range(4):
-                queue.dma_start(t[32 * q : 32 * q + 4, :].bitcast(I32), src[0, 4 * q : 4 * q + 4, :].bitcast(I32))
+        def load_plane(t, src, queues):
+            for q, queue in enumerate(queues):
+                queue.dma_start(t[32 * q : 32 * q + 4, 0 : src.shape[2]].bitcast(I32), src[0, 4 * q : 4 * q + 4, :].bitcast(I32))
 
-        def zeroed_halves(name):
-            t = tile(name, 2 * R, U8)
+        def zeroed_halves(name, count):
+            t = tile(name, 2 * count * R + 4, U8)
             nc.vector.memset(t[0:64, :].bitcast(I32), 0)
             return t
 
-        def load_halves(t, src):
-            rows = src[0].bitcast(I32).rearrange("(h q r) c -> q r h c", h=2, q=2)
-            for q in range(2):
-                nc.sync.dma_start(t[32 * q : 32 * q + 4, :].bitcast(I32).rearrange("p (h c) -> p h c", h=2), rows[q])
+        def load_halves(t, srcs):
+            count = len(srcs)
+            for w, src in enumerate(srcs):
+                rows = src[0].bitcast(I32).rearrange("(h q r) c -> q r h c", h=2, q=2)
+                for q in range(2):
+                    dst = t[32 * q : 32 * q + 4, 0 : 2 * count * R].bitcast(I32).rearrange("p (w h c) -> p w h c", h=2, w=count)
+                    nc.sync.dma_start(dst[:, w, :, :], rows[q])
 
-        def gather(name, window, offsets, dtype):
-            t = tile(name, J, dtype)
+        def gather(name, window, offsets, dtype, tag=None):
+            t = tile(name, J, dtype, tag)
             nc.vector.tensor_copy(t[:], window[:].indirect(offsets[:]))
             return t
 
@@ -77,39 +80,40 @@ def tile_list_owncommon_leaned_store_plain_kernel(
             nc.scalar.copy(t[:].rearrange("p (t m i) -> p m t i", t=PACK, i=i), src[:].rearrange("p (m i t) -> p m t i", t=PACK, i=i))
             return t
 
-        def deal_plane(name, src):
-            t = tile(name, R, U8)
-            nc.vector.tensor_copy(src[64:128, 0:R].bitcast(I32), src[0:64, R : 2 * R].bitcast(I32))
-            nc.vector.tensor_copy(t[:].rearrange("p (t m) -> p t m", t=PACK), src[:, 0:R].rearrange("p (m t) -> p t m", t=PACK))
+        def deal_planes(name, src, count):
+            width = count * R
+            t = tile(name, width, U8)
+            nc.vector.tensor_copy(src[64:128, 0 : 2 * width - R].bitcast(I32), src[0:64, R : 2 * width].bitcast(I32))
+            nc.vector.tensor_copy(
+                t[:].rearrange("p (w t m) -> p w t m", w=count, t=PACK), src[:, 0 : 2 * width].rearrange("p (w h m t) -> p w h t m", w=count, h=2, t=PACK)[:, :, 0, :, :]
+            )
             return t
 
-        w_s = zeroed_halves("w_s")
-        xt_s = zeroed_plane("xt_s", T)
-        w2_s = zeroed_halves("w2_s")
-        w0_s = zeroed_halves("w0_s")
+        w_s = zeroed_halves("w_s", 1)
+        xt_s = zeroed_plane("xt_s", T, nc.gpsimd)
+        wb_s = zeroed_halves("wb_s", 2)
         xo_s = zeroed_plane("xo_s", Z)
-        vs_s = zeroed_plane("vs_s", S)
         pw = [tile("pw%d" % i, C, F32) for i in range(2)]
-        pv = [tile("pv%d" % i, D, F32) for i in range(4)]
+        pv = [tile("pv%d" % i, D, F32) for i in range(2)]
         for b in pw + pv:
-            nc.vector.memset(b[:].bitcast(I32), 0)
+            nc.gpsimd.memset(b[:].bitcast(I32), 0)
+        vs_s = zeroed_plane("vs_s", S, nc.gpsimd)
 
         sa_t = keep.tile([P, PACK], F32, name="sa_t")
         sb_t = keep.tile([P, PACK], F32, name="sb_t")
         l1 = load_list("l1", offs)
-        load_halves(w_s, w_scales)
-        load_plane(xt_s, xt_scales, nc.scalar)
+        load_halves(w_s, [w_scales])
+        load_plane(xt_s, xt_scales, [nc.scalar] * 3 + [nc.sync])
         xt_w = load_words8("xt_w", xt_words, T)
         w_w = load_words4("w_w", w_words, R)
-        load_halves(w2_s, w2_scales)
-        load_halves(w0_s, w0_scales)
         w2_w = load_words8("w2_w", w2_words, R)
         w0_w = load_words8("w0_w", w0_words, R, "w0_w")
-        xo_w = load_words4("xo_w", xo_words, Z)
+        load_halves(wb_s, [w2_scales, w0_scales])
         l3 = load_list("l3", offs3)
+        xo_w = load_words4("xo_w", xo_words, Z)
         l2 = load_list("l2", offs2)
-        load_plane(xo_s, xo_scales, nc.sync)
-        load_plane(vs_s, vs_scales, nc.gpsimd)
+        load_plane(xo_s, xo_scales, [nc.sync] * 4)
+        load_plane(vs_s, vs_scales, [nc.gpsimd] * 4)
         l4 = load_list("l4", offs4)
         vs_w = load_words8("vs_w", vs_words, S)
         l7 = load_list("l7", offs7)
@@ -120,8 +124,8 @@ def tile_list_owncommon_leaned_store_plain_kernel(
 
         w_wd = deal_words("w_wd", w_w, U16)
         xt_sg = gather("xt_sg", xt_s, l1, U8)
-        w_sd = deal_plane("w_sd", w_s)
-        xt_wg = gather("xt_wg", xt_w, l1, U32)
+        w_sd = deal_planes("w_sd", w_s, 1)
+        xt_wg = gather("xt_wg", xt_w, l1, U32, "xt_s")
         w2_wd = deal_words("w2_wd", w2_w, U32)
         w0_wd = deal_words("w0_wd", w0_w, U32)
 
@@ -134,46 +138,50 @@ def tile_list_owncommon_leaned_store_plain_kernel(
                 rhs=xt_wg[:].bitcast(E4M3), rhs_scale=xt_sg[:], start=True, stop=True,
             )
 
-        w2_sd = deal_plane("w2_sd", w2_s)
-        w0_sd = deal_plane("w0_sd", w0_s)
+        wb_sd = deal_planes("wb_sd", wb_s, 2)
         xo_wg = gather("xo_wg", xo_w, l2, U16)
         xo_sg = gather("xo_sg", xo_s, l2, U8)
+        for name, tag in (("pv2", "xo_w"), ("pv3", "xo_s")):
+            b = tile(name, D, F32, tag)
+            nc.gpsimd.memset(b[:].bitcast(I32), 0)
+            pv.append(b)
         vs_wg = gather("vs_wg", vs_w, l7, U32)
-        vs_sg = gather("vs_sg", vs_s, l7, U8)
         for t in range(PACK):
             cols = slice(P * t, P * (t + 1))
             nc.tensor.matmul_mx(
-                out=b_ps[t][:], lhsT=w2_wd[:, cols].bitcast(E5M2), lhsT_scale=w2_sd[:, cols],
+                out=b_ps[t][:], lhsT=w2_wd[:, cols].bitcast(E5M2), lhsT_scale=wb_sd[:, cols],
                 rhs=xt_wg[:].bitcast(E4M3), rhs_scale=xt_sg[:], start=True, stop=False,
             )
             nc.tensor.matmul_mx(
-                out=b_ps[t][:], lhsT=w0_wd[:, cols].bitcast(E5M2), lhsT_scale=w0_sd[:, cols],
+                out=b_ps[t][:], lhsT=w0_wd[:, cols].bitcast(E5M2), lhsT_scale=wb_sd[:, R + P * t : R + P * (t + 1)],
                 rhs=xo_wg[:].bitcast(E2M1), rhs_scale=xo_sg[:], start=False, stop=True,
             )
 
-        gw = [tile("gw%d" % t, O, F32) for t in range(PACK)]
-        gv = [tile("gv%d" % t, O, F32) for t in range(PACK)]
-        hid_t = keep.tile([P, PACK, O], BF16, name="hid_t", align_bytes=64)
+        gw = keep.tile([P, PACK, O], F32, name="gw", align_bytes=64)
+        gv = keep.tile([P, PACK, O], F32, name="gv", align_bytes=64)
         hid = keep.tile([P, O, PACK], BF16, name="hid", align_bytes=64)
 
-        a_sb = keep.tile([P, 2 * J], F32, name="a_sb", tag="w0_w", align_bytes=64)
+        a_sb = tile("a_sb", 2 * J, F32)
         for t in range(PACK):
             a_t = a_sb[:, (t % 2) * J : (t % 2 + 1) * J]
-            nc.scalar.activation(a_t, a_ps[t][:], COPY)
+            if t < 1:
+                nc.vector.tensor_copy(a_t, a_ps[t][:])
+            else:
+                nc.scalar.activation(a_t, a_ps[t][:], COPY)
             nc.scalar.activation(pw[t % 2][:].indirect(l3[:]), a_t, COPY)
-            nc.scalar.activation(gw[t][:], pw[t % 2][:].indirect(l5[:]), COPY, scale=sa_t[:, t : t + 1])
+            nc.scalar.activation(gw[:, t, :], pw[t % 2][:].indirect(l5[:]), COPY, scale=sa_t[:, t : t + 1])
 
         for t in range(PACK):
             b_sb = tile("b_sb%d" % t, J, F32)
-            if t == PACK - 1:
+            if t >= 2:
                 nc.scalar.activation(b_sb[:], b_ps[t][:], COPY)
             else:
                 nc.vector.tensor_copy(b_sb[:], b_ps[t][:])
             nc.vector.tensor_copy(pv[t][:].indirect(l4[:]), b_sb[:])
-            nc.scalar.activation(gv[t][:], pv[t][:].indirect(l6[:]), COPY, scale=sb_t[:, t : t + 1])
-            nc.vector.tensor_tensor(hid_t[:, t, :], gw[t][:], gv[t][:], MAX)
+            nc.scalar.activation(gv[:, t, :], pv[t][:].indirect(l6[:]), COPY, scale=sb_t[:, t : t + 1])
 
-        nc.vector.tensor_copy(hid[:], hid_t[:].rearrange("p t o -> p o t"))
+        vs_sg = gather("vs_sg", vs_s, l7, U8, "b_sb%d" % (PACK - 1))
+        nc.vector.tensor_tensor(hid[:], gw[:].rearrange("p t o -> p o t"), gv[:].rearrange("p t o -> p o t"), MAX)
         hid_w = tile("hid_w", O, U32)
         hid_s = tile("hid_s", O, U8)
         nc.vector.quantize_mx(out=hid_w[:].bitcast(E4M3), scales=hid_s[:], in_=hid[:].rearrange("p o t -> p (o t)"))

@@ -15,9 +15,15 @@ COPY = mybir.ActivationFunctionType.Copy
 MAX = mybir.AluOpType.max
 
 P = 128
+HALF = P // 2
+QUAD = 32
+LIVE = 4
 PACK = 4
 T, J, R, Z, C, D, O, N, S = 1024, 256, 512, 1024, 512, 512, 128, 256, 1024
-FLOPS = 436207616
+FLOPS = 2 * 512 * (3 * R * J + N * O)
+
+SPARE = 4
+B_ON_SCALAR_FROM = 2
 
 
 def tile_list_owncommon_leaned_store_plain_kernel(
@@ -29,174 +35,177 @@ def tile_list_owncommon_leaned_store_plain_kernel(
         keep = ctx.enter_context(tc.tile_pool(name="keep", bufs=1))
         psum = ctx.enter_context(tc.psum_pool(name="psum", bufs=1))
 
-        def tile(name, width, dtype, tag=None):
-            return keep.tile([P, width], dtype, name=name, tag=tag or name, align_bytes=64)
+        def tile(name, width, dtype, on=None):
+            return keep.tile([P, width], dtype, name=name, tag=on or name, align_bytes=64)
+
+        def zeroed(engine, name, width, dtype, on=None):
+            fresh = tile(name, width, dtype, on)
+            engine.memset(fresh[:].bitcast(I32), 0)
+            return fresh
 
         def load_list(name, src):
-            t = keep.tile([P, src.shape[1]], U16, name=name)
-            nc.sync.dma_start(t[:], src)
-            return t
+            offsets = keep.tile([P, src.shape[1]], U16, name=name)
+            nc.sync.dma_start(offsets[:], src)
+            return offsets
 
-        def load_words8(name, src, width, tag=None, queue=nc.sync):
-            t = keep.tile([P, width], U32, name=name, tag=tag or name, align_bytes=64)
-            queue.dma_start(t[:].bitcast(I32), src[0].rearrange("p n t -> p (n t)").bitcast(I32))
-            return t
+        def load_fp8_words(name, src, width):
+            words = tile(name, width, U32)
+            nc.sync.dma_start(words[:].bitcast(I32), src[0].rearrange("p n t -> p (n t)").bitcast(I32))
+            return words
 
-        def load_words4(name, src, width, queue=nc.sync):
-            t = tile(name, width, U16)
-            queue.dma_start(t[:].bitcast(I32), src[0].bitcast(I32))
-            return t
+        def load_fp4_words(name, src, width):
+            words = tile(name, width, U16)
+            nc.sync.dma_start(words[:].bitcast(I32), src[0].bitcast(I32))
+            return words
 
-        def zeroed_plane(name, width, eng=nc.vector):
-            t = tile(name, width + 4, U8)
-            eng.memset(t[:].bitcast(I32), 0)
-            return t
+        def load_per_row(dst, src):
+            nc.sync.dma_start(dst[:], src.rearrange("(p t) o -> p (t o)", t=PACK))
 
-        def load_plane(t, src, queues):
+        def load_plane(plane, src, queues):
+            width = src.shape[2]
             for q, queue in enumerate(queues):
-                queue.dma_start(t[32 * q : 32 * q + 4, 0 : src.shape[2]].bitcast(I32), src[0, 4 * q : 4 * q + 4, :].bitcast(I32))
+                rows = src[0, LIVE * q : LIVE * (q + 1), :]
+                queue.dma_start(plane[QUAD * q : QUAD * q + LIVE, 0:width].bitcast(I32), rows.bitcast(I32))
 
-        def zeroed_halves(name, count):
-            t = tile(name, 2 * count * R + 4, U8)
-            nc.vector.memset(t[0:64, :].bitcast(I32), 0)
-            return t
+        def zeroed_landing(name, weights):
+            landing = tile(name, 2 * weights * R + SPARE, U8)
+            nc.vector.memset(landing[0:HALF, :].bitcast(I32), 0)
+            return landing
 
-        def load_halves(t, srcs):
-            count = len(srcs)
+        def load_landing(landing, srcs):
+            ranges = landing[:, 0 : 2 * len(srcs) * R].bitcast(I32).rearrange("p (w h c) -> p w h c", w=len(srcs), h=2)
             for w, src in enumerate(srcs):
-                rows = src[0].bitcast(I32).rearrange("(h q r) c -> q r h c", h=2, q=2)
+                rows = src[0].bitcast(I32).rearrange("(h q s) c -> q s h c", h=2, q=2)
                 for q in range(2):
-                    dst = t[32 * q : 32 * q + 4, 0 : 2 * count * R].bitcast(I32).rearrange("p (w h c) -> p w h c", h=2, w=count)
-                    nc.sync.dma_start(dst[:, w, :, :], rows[q])
+                    nc.sync.dma_start(ranges[QUAD * q : QUAD * q + LIVE, w, :, :], rows[q])
 
-        def gather(name, window, offsets, dtype, tag=None):
-            t = tile(name, J, dtype, tag)
-            nc.vector.tensor_copy(t[:], window[:].indirect(offsets[:]))
-            return t
+        def deal_planes(name, landing, weights):
+            width = weights * R
+            dealt = tile(name, width, U8)
+            nc.vector.tensor_copy(landing[HALF:P, 0 : 2 * width - R].bitcast(I32), landing[0:HALF, R : 2 * width].bitcast(I32))
+            planes = landing[:, 0 : 2 * width].rearrange("p (w h m t) -> p w h t m", w=weights, h=2, t=PACK)[:, :, 0, :, :]
+            nc.vector.tensor_copy(dealt[:].rearrange("p (w t m) -> p w t m", w=weights, t=PACK), planes)
+            return dealt
 
-        def deal_words(name, src, dtype):
-            t = tile(name, R, dtype)
-            i = 4 if dtype == U32 else 8
-            nc.scalar.copy(t[:].rearrange("p (t m i) -> p m t i", t=PACK, i=i), src[:].rearrange("p (m i t) -> p m t i", t=PACK, i=i))
-            return t
-
-        def deal_planes(name, src, count):
-            width = count * R
-            t = tile(name, width, U8)
-            nc.vector.tensor_copy(src[64:128, 0 : 2 * width - R].bitcast(I32), src[0:64, R : 2 * width].bitcast(I32))
-            nc.vector.tensor_copy(
-                t[:].rearrange("p (w t m) -> p w t m", w=count, t=PACK), src[:, 0 : 2 * width].rearrange("p (w h m t) -> p w h t m", w=count, h=2, t=PACK)[:, :, 0, :, :]
+        def deal_words(name, words, dtype, copy):
+            dealt = tile(name, R, dtype)
+            run = 4 if dtype == U32 else 8
+            copy(
+                dealt[:].rearrange("p (t m i) -> p m t i", t=PACK, i=run),
+                words[:].rearrange("p (m i t) -> p m t i", t=PACK, i=run),
             )
-            return t
+            return dealt
 
-        w_s = zeroed_halves("w_s", 1)
-        xt_s = zeroed_plane("xt_s", T, nc.gpsimd)
-        wb_s = zeroed_halves("wb_s", 2)
-        xo_s = zeroed_plane("xo_s", Z)
-        pw = [tile("pw%d" % i, C, F32) for i in range(2)]
-        pv = [tile("pv%d" % i, D, F32) for i in range(2)]
-        for b in pw + pv:
-            nc.gpsimd.memset(b[:].bitcast(I32), 0)
-        vs_s = zeroed_plane("vs_s", S, nc.gpsimd)
+        def gather(name, window, offsets, dtype, on=None):
+            picked = tile(name, J, dtype, on)
+            nc.vector.tensor_copy(picked[:], window[:].indirect(offsets[:]))
+            return picked
 
-        sa_t = keep.tile([P, PACK], F32, name="sa_t")
-        sb_t = keep.tile([P, PACK], F32, name="sb_t")
-        l1 = load_list("l1", offs)
-        load_halves(w_s, [w_scales])
-        load_plane(xt_s, xt_scales, [nc.scalar] * 3 + [nc.sync])
-        xt_w = load_words8("xt_w", xt_words, T)
-        w_w = load_words4("w_w", w_words, R)
-        w2_w = load_words8("w2_w", w2_words, R)
-        w0_w = load_words8("w0_w", w0_words, R, "w0_w")
-        load_halves(wb_s, [w2_scales, w0_scales])
-        l3 = load_list("l3", offs3)
-        xo_w = load_words4("xo_w", xo_words, Z)
-        l2 = load_list("l2", offs2)
-        load_plane(xo_s, xo_scales, [nc.sync] * 4)
-        load_plane(vs_s, vs_scales, [nc.gpsimd] * 4)
-        l4 = load_list("l4", offs4)
-        vs_w = load_words8("vs_w", vs_words, S)
-        l7 = load_list("l7", offs7)
-        l5 = load_list("l5", offs5)
-        nc.sync.dma_start(sa_t[:], sa.rearrange("(p t) o -> p (t o)", t=PACK))
-        l6 = load_list("l6", offs6)
-        nc.sync.dma_start(sb_t[:], sb.rearrange("(p t) o -> p (t o)", t=PACK))
+        w_landing = zeroed_landing("w_landing", 1)
+        xt_plane = zeroed(nc.gpsimd, "xt_plane", T, U8)
+        w2_w0_landing = zeroed_landing("w2_w0_landing", 2)
+        xo_plane = zeroed(nc.vector, "xo_plane", Z + SPARE, U8)
+        pw = [zeroed(nc.vector, "pw%d" % i, C, F32) for i in range(2)]
+        pv = [zeroed(nc.gpsimd, "pv%d" % i, D, F32) for i in range(2)]
+        vs_plane = zeroed(nc.gpsimd, "vs_plane", S, U8)
 
-        w_wd = deal_words("w_wd", w_w, U16)
-        xt_sg = gather("xt_sg", xt_s, l1, U8)
-        w_sd = deal_planes("w_sd", w_s, 1)
-        xt_wg = gather("xt_wg", xt_w, l1, U32, "xt_s")
-        w2_wd = deal_words("w2_wd", w2_w, U32)
-        w0_wd = deal_words("w0_wd", w0_w, U32)
+        sa_rows = keep.tile([P, PACK], F32, name="sa_rows")
+        sb_rows = keep.tile([P, PACK], F32, name="sb_rows")
+        idx = load_list("idx", offs)
+        load_landing(w_landing, [w_scales])
+        load_plane(xt_plane, xt_scales, [nc.scalar] * 3 + [nc.sync])
+        xt_w = load_fp8_words("xt_w", xt_words, T)
+        w_w = load_fp4_words("w_w", w_words, R)
+        w2_w = load_fp8_words("w2_w", w2_words, R)
+        load_landing(w2_w0_landing, [w2_scales, w0_scales])
+        w0_w = load_fp8_words("w0_w", w0_words, R)
+        xo_w = load_fp4_words("xo_w", xo_words, Z)
+        idx3 = load_list("idx3", offs3)
+        idx2 = load_list("idx2", offs2)
+        load_plane(xo_plane, xo_scales, [nc.sync] * 4)
+        idx4 = load_list("idx4", offs4)
+        vs_w = load_fp8_words("vs_w", vs_words, S)
+        idx7 = load_list("idx7", offs7)
+        idx5 = load_list("idx5", offs5)
+        load_per_row(sa_rows, sa)
+        load_plane(vs_plane, vs_scales, [nc.sync] * 4)
+        idx6 = load_list("idx6", offs6)
+        load_per_row(sb_rows, sb)
+
+        w_dealt = deal_words("w_dealt", w_w, U16, nc.scalar.copy)
+        xt_sel_plane = gather("xt_sel_plane", xt_plane, idx, U8)
+        w_plane = deal_planes("w_plane", w_landing, 1)
+        xt_sel = gather("xt_sel", xt_w, idx, U32, on="xt_plane")
+        w2_dealt = deal_words("w2_dealt", w2_w, U32, nc.scalar.copy)
 
         a_ps = [psum.tile([P, J], F32, name="a_ps%d" % t, tag="bank%d" % t) for t in range(PACK)]
         b_ps = [psum.tile([P, J], F32, name="b_ps%d" % t, tag="bank%d" % (PACK + t)) for t in range(PACK)]
         for t in range(PACK):
             cols = slice(P * t, P * (t + 1))
             nc.tensor.matmul_mx(
-                out=a_ps[t][:], lhsT=w_wd[:, cols].bitcast(E2M1), lhsT_scale=w_sd[:, cols],
-                rhs=xt_wg[:].bitcast(E4M3), rhs_scale=xt_sg[:], start=True, stop=True,
+                out=a_ps[t][:], lhsT=w_dealt[:, cols].bitcast(E2M1), lhsT_scale=w_plane[:, cols],
+                rhs=xt_sel[:].bitcast(E4M3), rhs_scale=xt_sel_plane[:], start=True, stop=True,
             )
 
-        wb_sd = deal_planes("wb_sd", wb_s, 2)
-        xo_wg = gather("xo_wg", xo_w, l2, U16)
-        xo_sg = gather("xo_sg", xo_s, l2, U8)
-        for name, tag in (("pv2", "xo_w"), ("pv3", "xo_s")):
-            b = tile(name, D, F32, tag)
-            nc.gpsimd.memset(b[:].bitcast(I32), 0)
-            pv.append(b)
-        vs_wg = gather("vs_wg", vs_w, l7, U32)
+        w2_w0_planes = deal_planes("w2_w0_planes", w2_w0_landing, 2)
+        w0_dealt = deal_words("w0_dealt", w0_w, U32, nc.vector.tensor_copy)
+        xo_sel = gather("xo_sel", xo_w, idx2, U16)
+        xo_sel_plane = gather("xo_sel_plane", xo_plane, idx2, U8)
+        pv.append(zeroed(nc.gpsimd, "pv2", D, F32, on="xo_w"))
+        pv.append(zeroed(nc.gpsimd, "pv3", D, F32, on="xo_plane"))
+        vs_sel = gather("vs_sel", vs_w, idx7, U32)
         for t in range(PACK):
             cols = slice(P * t, P * (t + 1))
+            w0_plane_cols = slice(R + P * t, R + P * (t + 1))
             nc.tensor.matmul_mx(
-                out=b_ps[t][:], lhsT=w2_wd[:, cols].bitcast(E5M2), lhsT_scale=wb_sd[:, cols],
-                rhs=xt_wg[:].bitcast(E4M3), rhs_scale=xt_sg[:], start=True, stop=False,
+                out=b_ps[t][:], lhsT=w2_dealt[:, cols].bitcast(E5M2), lhsT_scale=w2_w0_planes[:, cols],
+                rhs=xt_sel[:].bitcast(E4M3), rhs_scale=xt_sel_plane[:], start=True, stop=False,
             )
             nc.tensor.matmul_mx(
-                out=b_ps[t][:], lhsT=w0_wd[:, cols].bitcast(E5M2), lhsT_scale=wb_sd[:, R + P * t : R + P * (t + 1)],
-                rhs=xo_wg[:].bitcast(E2M1), rhs_scale=xo_sg[:], start=False, stop=True,
+                out=b_ps[t][:], lhsT=w0_dealt[:, cols].bitcast(E5M2), lhsT_scale=w2_w0_planes[:, w0_plane_cols],
+                rhs=xo_sel[:].bitcast(E2M1), rhs_scale=xo_sel_plane[:], start=False, stop=True,
             )
 
-        gw = keep.tile([P, PACK, O], F32, name="gw", align_bytes=64)
-        gv = keep.tile([P, PACK, O], F32, name="gv", align_bytes=64)
+        pw_picked = keep.tile([P, PACK, O], F32, name="pw_picked", align_bytes=64)
+        pv_picked = keep.tile([P, PACK, O], F32, name="pv_picked", align_bytes=64)
         hid = keep.tile([P, O, PACK], BF16, name="hid", align_bytes=64)
 
         a_sb = tile("a_sb", 2 * J, F32)
         for t in range(PACK):
             a_t = a_sb[:, (t % 2) * J : (t % 2 + 1) * J]
-            if t < 1:
-                nc.vector.tensor_copy(a_t, a_ps[t][:])
-            else:
-                nc.scalar.activation(a_t, a_ps[t][:], COPY)
-            nc.scalar.activation(pw[t % 2][:].indirect(l3[:]), a_t, COPY)
-            nc.scalar.activation(gw[:, t, :], pw[t % 2][:].indirect(l5[:]), COPY, scale=sa_t[:, t : t + 1])
+            nc.scalar.activation(a_t, a_ps[t][:], COPY)
+            nc.scalar.activation(pw[t % 2][:].indirect(idx3[:]), a_t, COPY)
+            nc.scalar.activation(pw_picked[:, t, :], pw[t % 2][:].indirect(idx5[:]), COPY, scale=sa_rows[:, t : t + 1])
 
         for t in range(PACK):
-            b_sb = tile("b_sb%d" % t, J, F32)
-            if t >= 2:
-                nc.scalar.activation(b_sb[:], b_ps[t][:], COPY)
+            b_t = tile("b_sb%d" % t, J, F32)
+            if t >= B_ON_SCALAR_FROM:
+                nc.scalar.activation(b_t[:], b_ps[t][:], COPY)
             else:
-                nc.vector.tensor_copy(b_sb[:], b_ps[t][:])
-            nc.vector.tensor_copy(pv[t][:].indirect(l4[:]), b_sb[:])
-            nc.scalar.activation(gv[:, t, :], pv[t][:].indirect(l6[:]), COPY, scale=sb_t[:, t : t + 1])
+                nc.vector.tensor_copy(b_t[:], b_ps[t][:])
+            nc.vector.tensor_copy(pv[t][:].indirect(idx4[:]), b_t[:])
+            nc.scalar.activation(pv_picked[:, t, :], pv[t][:].indirect(idx6[:]), COPY, scale=sb_rows[:, t : t + 1])
 
-        vs_sg = gather("vs_sg", vs_s, l7, U8, "b_sb%d" % (PACK - 1))
-        nc.vector.tensor_tensor(hid[:], gw[:].rearrange("p t o -> p o t"), gv[:].rearrange("p t o -> p o t"), MAX)
-        hid_w = tile("hid_w", O, U32)
-        hid_s = tile("hid_s", O, U8)
-        nc.vector.quantize_mx(out=hid_w[:].bitcast(E4M3), scales=hid_s[:], in_=hid[:].rearrange("p o t -> p (o t)"))
+        vs_sel_plane = gather("vs_sel_plane", vs_plane, idx7, U8, on="b_sb%d" % (PACK - 1))
 
-        for h in range(2):
-            cols = slice(P * h, P * (h + 1))
+        nc.vector.tensor_tensor(
+            hid[:].rearrange("p (c i) t -> p c t i", i=2),
+            pw_picked[:].rearrange("p t (c i) -> p c t i", i=2),
+            pv_picked[:].rearrange("p t (c i) -> p c t i", i=2),
+            MAX,
+        )
+        hid_words = tile("hid_words", O, U32)
+        hid_plane = tile("hid_plane", O, U8)
+        nc.vector.quantize_mx(out=hid_words[:].bitcast(E4M3), scales=hid_plane[:], in_=hid[:].rearrange("p o t -> p (o t)"))
+
+        leave = ((lambda dst, src: nc.scalar.activation(dst, src, COPY), nc.scalar), (nc.vector.tensor_copy, nc.sync))
+        for h, (empty_bank, queue) in enumerate(leave):
+            rows = slice(P * h, P * (h + 1))
             y_ps = psum.tile([P, O], F32, name="y_ps%d" % h, tag="bank%d" % h)
             nc.tensor.matmul_mx(
-                out=y_ps[:], lhsT=vs_wg[:, cols].bitcast(E5M2), lhsT_scale=vs_sg[:, cols],
-                rhs=hid_w[:].bitcast(E4M3), rhs_scale=hid_s[:], start=True, stop=True,
+                out=y_ps[:], lhsT=vs_sel[:, rows].bitcast(E5M2), lhsT_scale=vs_sel_plane[:, rows],
+                rhs=hid_words[:].bitcast(E4M3), rhs_scale=hid_plane[:], start=True, stop=True,
             )
             y_sb = tile("y_sb%d" % h, O, F32)
-            if h == 0:
-                nc.scalar.activation(y_sb[:], y_ps[:], COPY)
-                nc.scalar.dma_start(out[cols, :], y_sb[:])
-            else:
-                nc.vector.tensor_copy(y_sb[:], y_ps[:])
-                nc.sync.dma_start(out[cols, :], y_sb[:])
+            empty_bank(y_sb[:], y_ps[:])
+            queue.dma_start(out[rows, :], y_sb[:])

from contextlib import ExitStack

import concourse.mybir as mybir

F32 = mybir.dt.float32
BF16 = mybir.dt.bfloat16
I32 = mybir.dt.int32
U32 = mybir.dt.uint32
U16 = mybir.dt.uint16
U8 = mybir.dt.uint8
E4M3 = mybir.dt.float8_e4m3fn_x4
E5M2 = mybir.dt.float8_e5m2_x4
E2M1 = mybir.dt.float4_e2m1fn_x4
COPY = mybir.ActivationFunctionType.Copy
MAX = mybir.AluOpType.max

P = 128
HALF = P // 2
QUAD = 32
LIVE = 4
PACK = 4
T, J, R, Z, C, D, O, N, S = 1024, 256, 512, 1024, 512, 512, 128, 256, 1024
FLOPS = 2 * 512 * (3 * R * J + N * O)

SPARE = 4
B_ON_SCALAR_FROM = 2


def tile_list_owncommon_leaned_store_plain_kernel(
    tc, xt_words, xt_scales, xo_words, xo_scales, w_words, w_scales, w2_words, w2_scales, w0_words, w0_scales,
    sa, sb, vs_words, vs_scales, offs, offs2, offs3, offs4, offs5, offs6, offs7, out,
):
    nc = tc.nc
    with ExitStack() as ctx:
        keep = ctx.enter_context(tc.tile_pool(name="keep", bufs=1))
        psum = ctx.enter_context(tc.psum_pool(name="psum", bufs=1))

        def tile(name, width, dtype, on=None):
            return keep.tile([P, width], dtype, name=name, tag=on or name, align_bytes=64)

        def zeroed(engine, name, width, dtype, on=None):
            fresh = tile(name, width, dtype, on)
            engine.memset(fresh[:].bitcast(I32), 0)
            return fresh

        def load_list(name, src):
            offsets = keep.tile([P, src.shape[1]], U16, name=name)
            nc.sync.dma_start(offsets[:], src)
            return offsets

        def load_fp8_words(name, src, width):
            words = tile(name, width, U32)
            nc.sync.dma_start(words[:].bitcast(I32), src[0].rearrange("p n t -> p (n t)").bitcast(I32))
            return words

        def load_fp4_words(name, src, width):
            words = tile(name, width, U16)
            nc.sync.dma_start(words[:].bitcast(I32), src[0].bitcast(I32))
            return words

        def load_per_row(dst, src):
            nc.sync.dma_start(dst[:], src.rearrange("(p t) o -> p (t o)", t=PACK))

        def load_plane(plane, src, queues):
            width = src.shape[2]
            for q, queue in enumerate(queues):
                rows = src[0, LIVE * q : LIVE * (q + 1), :]
                queue.dma_start(plane[QUAD * q : QUAD * q + LIVE, 0:width].bitcast(I32), rows.bitcast(I32))

        def zeroed_landing(name, weights):
            landing = tile(name, 2 * weights * R + SPARE, U8)
            nc.vector.memset(landing[0:HALF, :].bitcast(I32), 0)
            return landing

        def load_landing(landing, srcs):
            ranges = landing[:, 0 : 2 * len(srcs) * R].bitcast(I32).rearrange("p (w h c) -> p w h c", w=len(srcs), h=2)
            for w, src in enumerate(srcs):
                rows = src[0].bitcast(I32).rearrange("(h q s) c -> q s h c", h=2, q=2)
                for q in range(2):
                    nc.sync.dma_start(ranges[QUAD * q : QUAD * q + LIVE, w, :, :], rows[q])

        def deal_planes(name, landing, weights):
            width = weights * R
            dealt = tile(name, width, U8)
            nc.vector.tensor_copy(landing[HALF:P, 0 : 2 * width - R].bitcast(I32), landing[0:HALF, R : 2 * width].bitcast(I32))
            planes = landing[:, 0 : 2 * width].rearrange("p (w h m t) -> p w h t m", w=weights, h=2, t=PACK)[:, :, 0, :, :]
            nc.vector.tensor_copy(dealt[:].rearrange("p (w t m) -> p w t m", w=weights, t=PACK), planes)
            return dealt

        def deal_words(name, words, dtype, copy):
            dealt = tile(name, R, dtype)
            run = 4 if dtype == U32 else 8
            copy(
                dealt[:].rearrange("p (t m i) -> p m t i", t=PACK, i=run),
                words[:].rearrange("p (m i t) -> p m t i", t=PACK, i=run),
            )
            return dealt

        def gather(name, window, offsets, dtype, on=None):
            picked = tile(name, J, dtype, on)
            nc.vector.tensor_copy(picked[:], window[:].indirect(offsets[:]))
            return picked

        w_landing = zeroed_landing("w_landing", 1)
        xt_plane = zeroed(nc.gpsimd, "xt_plane", T, U8)
        w2_w0_landing = zeroed_landing("w2_w0_landing", 2)
        xo_plane = zeroed(nc.vector, "xo_plane", Z + SPARE, U8)
        pw = [zeroed(nc.vector, "pw%d" % i, C, F32) for i in range(2)]
        pv = [zeroed(nc.gpsimd, "pv%d" % i, D, F32) for i in range(2)]
        vs_plane = zeroed(nc.gpsimd, "vs_plane", S, U8)

        sa_rows = keep.tile([P, PACK], F32, name="sa_rows")
        sb_rows = keep.tile([P, PACK], F32, name="sb_rows")
        idx = load_list("idx", offs)
        load_landing(w_landing, [w_scales])
        load_plane(xt_plane, xt_scales, [nc.scalar] * 3 + [nc.sync])
        xt_w = load_fp8_words("xt_w", xt_words, T)
        w_w = load_fp4_words("w_w", w_words, R)
        w2_w = load_fp8_words("w2_w", w2_words, R)
        load_landing(w2_w0_landing, [w2_scales, w0_scales])
        w0_w = load_fp8_words("w0_w", w0_words, R)
        xo_w = load_fp4_words("xo_w", xo_words, Z)
        idx3 = load_list("idx3", offs3)
        idx2 = load_list("idx2", offs2)
        load_plane(xo_plane, xo_scales, [nc.sync] * 4)
        idx4 = load_list("idx4", offs4)
        vs_w = load_fp8_words("vs_w", vs_words, S)
        idx7 = load_list("idx7", offs7)
        idx5 = load_list("idx5", offs5)
        load_per_row(sa_rows, sa)
        load_plane(vs_plane, vs_scales, [nc.sync] * 4)
        idx6 = load_list("idx6", offs6)
        load_per_row(sb_rows, sb)

        w_dealt = deal_words("w_dealt", w_w, U16, nc.scalar.copy)
        xt_sel_plane = gather("xt_sel_plane", xt_plane, idx, U8)
        w_plane = deal_planes("w_plane", w_landing, 1)
        xt_sel = gather("xt_sel", xt_w, idx, U32, on="xt_plane")
        w2_dealt = deal_words("w2_dealt", w2_w, U32, nc.scalar.copy)

        a_ps = [psum.tile([P, J], F32, name="a_ps%d" % t, tag="bank%d" % t) for t in range(PACK)]
        b_ps = [psum.tile([P, J], F32, name="b_ps%d" % t, tag="bank%d" % (PACK + t)) for t in range(PACK)]
        for t in range(PACK):
            cols = slice(P * t, P * (t + 1))
            nc.tensor.matmul_mx(
                out=a_ps[t][:], lhsT=w_dealt[:, cols].bitcast(E2M1), lhsT_scale=w_plane[:, cols],
                rhs=xt_sel[:].bitcast(E4M3), rhs_scale=xt_sel_plane[:], start=True, stop=True,
            )

        w2_w0_planes = deal_planes("w2_w0_planes", w2_w0_landing, 2)
        w0_dealt = deal_words("w0_dealt", w0_w, U32, nc.vector.tensor_copy)
        xo_sel = gather("xo_sel", xo_w, idx2, U16)
        xo_sel_plane = gather("xo_sel_plane", xo_plane, idx2, U8)
        pv.append(zeroed(nc.gpsimd, "pv2", D, F32, on="xo_w"))
        pv.append(zeroed(nc.gpsimd, "pv3", D, F32, on="xo_plane"))
        vs_sel = gather("vs_sel", vs_w, idx7, U32)
        for t in range(PACK):
            cols = slice(P * t, P * (t + 1))
            w0_plane_cols = slice(R + P * t, R + P * (t + 1))
            nc.tensor.matmul_mx(
                out=b_ps[t][:], lhsT=w2_dealt[:, cols].bitcast(E5M2), lhsT_scale=w2_w0_planes[:, cols],
                rhs=xt_sel[:].bitcast(E4M3), rhs_scale=xt_sel_plane[:], start=True, stop=False,
            )
            nc.tensor.matmul_mx(
                out=b_ps[t][:], lhsT=w0_dealt[:, cols].bitcast(E5M2), lhsT_scale=w2_w0_planes[:, w0_plane_cols],
                rhs=xo_sel[:].bitcast(E2M1), rhs_scale=xo_sel_plane[:], start=False, stop=True,
            )

        pw_picked = keep.tile([P, PACK, O], F32, name="pw_picked", align_bytes=64)
        pv_picked = keep.tile([P, PACK, O], F32, name="pv_picked", align_bytes=64)
        hid = keep.tile([P, O, PACK], BF16, name="hid", align_bytes=64)

        a_sb = tile("a_sb", 2 * J, F32)
        for t in range(PACK):
            a_t = a_sb[:, (t % 2) * J : (t % 2 + 1) * J]
            nc.scalar.activation(a_t, a_ps[t][:], COPY)
            nc.scalar.activation(pw[t % 2][:].indirect(idx3[:]), a_t, COPY)
            nc.scalar.activation(pw_picked[:, t, :], pw[t % 2][:].indirect(idx5[:]), COPY, scale=sa_rows[:, t : t + 1])

        for t in range(PACK):
            b_t = tile("b_sb%d" % t, J, F32)
            if t >= B_ON_SCALAR_FROM:
                nc.scalar.activation(b_t[:], b_ps[t][:], COPY)
            else:
                nc.vector.tensor_copy(b_t[:], b_ps[t][:])
            nc.vector.tensor_copy(pv[t][:].indirect(idx4[:]), b_t[:])
            nc.scalar.activation(pv_picked[:, t, :], pv[t][:].indirect(idx6[:]), COPY, scale=sb_rows[:, t : t + 1])

        vs_sel_plane = gather("vs_sel_plane", vs_plane, idx7, U8, on="b_sb%d" % (PACK - 1))

        nc.vector.tensor_tensor(
            hid[:].rearrange("p (c i) t -> p c t i", i=2),
            pw_picked[:].rearrange("p t (c i) -> p c t i", i=2),
            pv_picked[:].rearrange("p t (c i) -> p c t i", i=2),
            MAX,
        )
        hid_words = tile("hid_words", O, U32)
        hid_plane = tile("hid_plane", O, U8)
        nc.vector.quantize_mx(out=hid_words[:].bitcast(E4M3), scales=hid_plane[:], in_=hid[:].rearrange("p o t -> p (o t)"))

        leave = ((lambda dst, src: nc.scalar.activation(dst, src, COPY), nc.scalar), (nc.vector.tensor_copy, nc.sync))
        for h, (empty_bank, queue) in enumerate(leave):
            rows = slice(P * h, P * (h + 1))
            y_ps = psum.tile([P, O], F32, name="y_ps%d" % h, tag="bank%d" % h)
            nc.tensor.matmul_mx(
                out=y_ps[:], lhsT=vs_sel[:, rows].bitcast(E5M2), lhsT_scale=vs_sel_plane[:, rows],
                rhs=hid_words[:].bitcast(E4M3), rhs_scale=hid_plane[:], start=True, stop=True,
            )
            y_sb = tile("y_sb%d" % h, O, F32)
            empty_bank(y_sb[:], y_ps[:])
            queue.dma_start(out[rows, :], y_sb[:])
